import numpy as np
import ml_dtypes


def mxq(x, axis, fmt="e4m3"):
    dtype, down = {"e4m3": (ml_dtypes.float8_e4m3fn, 7), "e5m2": (ml_dtypes.float8_e5m2, 14)}[fmt]
    v = np.moveaxis(np.asarray(x, np.float32).astype(ml_dtypes.bfloat16).astype(np.float64), axis, -1)
    blocks = v.reshape(v.shape[:-1] + (-1, 32))
    amax = np.abs(blocks).max(-1, keepdims=True)
    byte = np.maximum(np.where(amax > 0, np.frexp(amax)[1] - 1 + 127, 0) - down, 1)
    scale = np.exp2(byte - 127.0)
    codes = (blocks / scale).astype(np.float32).astype(dtype).astype(np.float64)
    return np.moveaxis((codes * scale).reshape(v.shape), -1, axis)


WIDE = False


def mx_kscale(k):
    if not WIDE:
        return np.ones(k)
    levels = np.array([10, -10, 5, -5, 0])
    if k % 512:
        return np.exp2(np.random.permutation(np.resize(levels, k // 32))).repeat(32)
    a = np.empty((k // 512, 16))
    for p in range(k // 512):
        a[p, :8] = np.random.permutation(np.resize(levels, 8))
        for g in range(8):
            far = levels[np.abs(levels - a[p, g]) >= 10]
            a[p, g + 8] = far[np.random.randint(len(far))]
    return np.exp2(a.ravel()).repeat(32)


BF16 = ml_dtypes.bfloat16


def bf(x):
    return np.asarray(x, np.float32).astype(BF16)


def f64(x):
    return np.asarray(x).astype(np.float64)


E2M1 = np.array([0.0, 0.5, 1.0, 1.5, 2.0, 3.0, 4.0, 6.0, -0.0, -0.5, -1.0, -1.5, -2.0, -3.0, -4.0, -6.0])


def pack_weight(w, fmt):
    k, n = w.shape
    w = f64(bf(w)).reshape(k // 32, 32, n)
    amax = np.abs(w).max(1)
    if fmt == "e4m3":
        byte = np.frexp(amax)[1] - 1 + 127 - 7
    else:
        mant, ex = np.frexp(amax / 6.0)
        byte = np.where(mant > 0.5, ex, ex - 1) + 127
    byte = np.clip(np.where(amax > 0, byte, 1), 1, 254)
    scaled = (w * np.exp2(127.0 - byte)[:, None, :]).reshape(k, n).astype(np.float32)
    by_word = np.ascontiguousarray(scaled.reshape(k // 512, 128, 4, n).transpose(0, 1, 3, 2))
    if fmt == "e4m3":
        words = by_word.astype(ml_dtypes.float8_e4m3fn).view(np.uint8)
    else:
        c = by_word.astype(ml_dtypes.float4_e2m1fn).view(np.uint8) & 0xF
        words = c[..., 0::2] | (c[..., 1::2] << 4)
    return np.ascontiguousarray(words), np.ascontiguousarray(byte.astype(np.uint8).reshape(k // 512, 16, n))


def unpack_weight(words, scales, fmt):
    g, p, n, _ = words.shape
    if fmt == "e4m3":
        vals = np.ascontiguousarray(words).view(ml_dtypes.float8_e4m3fn).astype(np.float64)
    else:
        nib = np.empty((g, p, n, 4), np.uint8)
        nib[..., 0::2] = words & 0xF
        nib[..., 1::2] = words >> 4
        vals = E2M1[nib]
    vals = vals * np.repeat(np.exp2(scales.astype(np.float64) - 127.0), 8, axis=1)[..., None]
    return vals.transpose(0, 1, 3, 2).reshape(g * 512, n)

E4M3FN = np.array([(-1.0 if i & 128 else 1.0) * ((1.0 + (i & 7) / 8.0) * 2.0 ** (((i >> 3) & 15) - 7) if i & 120 else (i & 7) * 2.0 ** -9) for i in range(256)])


def e4m3fn_bytes(y):
    return np.clip(np.asarray(y, np.float64), -448.0, 448.0).astype(np.float32).astype(ml_dtypes.float8_e4m3fn).view(np.uint8)


def e4m3fn_values(b):
    return E4M3FN[b]


B, N, D, H, F = 8, 16, 1024, 1024, 512


def lrelu(y):
    return np.maximum(y, 0.25 * y)


def draw0():
    s, t = mx_kscale(D), mx_kscale(H)
    x = bf(np.random.standard_normal((B, N, D)) * s)
    wa_words, wa_scales = pack_weight(np.random.standard_normal((D, H)) / np.sqrt(D) / s[:, None] * t, "e4m3")
    wb_words, wb_scales = pack_weight(np.random.standard_normal((D, H)) / np.sqrt(D) / s[:, None] * t, "e4m3")
    c = bf(np.random.standard_normal(H) * 0.3 * t)
    w2_words, w2_scales = pack_weight(np.random.standard_normal((H, F)) / np.sqrt(H) / t[:, None], "e4m3")
    return {
        "x": x,
        "wa_words": wa_words,
        "wa_scales": wa_scales,
        "wb_words": wb_words,
        "wb_scales": wb_scales,
        "c": c,
        "w2_words": w2_words,
        "w2_scales": w2_scales,
        "b2": bf(np.random.standard_normal(F) * 0.3),
        "v": bf(np.random.standard_normal(F) / np.sqrt(F)),
    }


def core(x, wa_words, wa_scales, wb_words, wb_scales, c, w2_words, w2_scales, b2, v):
    xq = mxq(f64(x).reshape(B * N, D), 1, "e4m3")
    a = (xq @ unpack_weight(wa_words, wa_scales, "e4m3")).reshape(B, N, H)
    g = (xq @ unpack_weight(wb_words, wb_scales, "e4m3")).reshape(B, N, H)
    z = lrelu(a[:, :, None, :] + g[:, None, :, :] + f64(c))
    y = mxq(z.reshape(B * N * N, H), 1, "e4m3") @ unpack_weight(w2_words, w2_scales, "e4m3")
    h = lrelu(y.reshape(B, N, N, F) + f64(b2))
    pooled = np.mean(h, axis=2)
    score = np.sum(pooled * f64(v), axis=-1)
    return pooled, score


def setup_inputs():
    drawn = draw0()
    full = np.asarray(drawn['x']).astype(np.float64)
    scale = (np.abs(full).reshape(8, 16, 8, 128).max(axis=(3,)) / 448.0).astype(np.float32)
    given = {}
    for key, value in drawn.items():
        if key == 'x':
            given['x_bytes'] = e4m3fn_bytes(full / np.repeat(scale.astype(np.float64), 128, axis=2))
            given['x_scale'] = scale
        else:
            given[key] = value
    return given


def reference(x_bytes, x_scale, wa_words, wa_scales, wb_words, wb_scales, c, w2_words, w2_scales, b2, v):
    return core(e4m3fn_values(x_bytes) * np.repeat(x_scale.astype(np.float64), 128, axis=2), wa_words, wa_scales, wb_words, wb_scales, c, w2_words, w2_scales, b2, v)

@@ -1,0 +1,367 @@
+from contextlib import ExitStack
+
+import concourse.mybir as mybir
+from concourse.masks import make_identity
+
+B, N, D, H, F = 8, 16, 1024, 1024, 512
+T = B * N
+FLOPS = 2 * T * D * H * 2 + 2 * B * N * N * H * F
+
+F32 = mybir.dt.float32
+BF16 = mybir.dt.bfloat16
+I32 = mybir.dt.int32
+U32 = mybir.dt.uint32
+U8 = mybir.dt.uint8
+FP8 = mybir.dt.float8_e4m3fn
+FP8X4 = mybir.dt.float8_e4m3fn_x4
+ALU = mybir.AluOpType
+ACT = mybir.ActivationFunctionType
+
+P = 128
+CHUNKS = [(0, 4), (4, 4), (8, 2), (10, 2), (12, 2), (14, 1), (15, 1)]
+QV = [12, 13]
+
+
+def tile_groupwisepairrankingscorer_d1p_kernel(
+    tc, x_bytes, x_scale, wa_words, wa_scales, wb_words, wb_scales, c, w2_words, w2_scales, b2, v, out_0, out_1
+):
+    nc = tc.nc
+    with ExitStack() as ctx:
+        keep = ctx.enter_context(tc.tile_pool(name="keep", bufs=1))
+        work = ctx.enter_context(tc.tile_pool(name="work", bufs=3))
+        psum = ctx.enter_context(tc.psum_pool(name="psum", bufs=1))
+        ctx.enter_context(tc.manual_schedule())
+
+        def bank(tag, shape, dtype, name, bufs=1):
+            return psum.tile(shape, dtype, tag=tag, name=name, bufs=bufs)
+
+        xs = keep.tile([P, 8], F32, name="xs")
+        xb = keep.tile([P, D], U8, name="xb", align_bytes=64)
+        nc.sync.dma_start(out=xs[:], in_=x_scale.rearrange("b n q -> (b n) q"))
+        nc.sync.dma_start(out=xb[:], in_=x_bytes.rearrange("b n k -> (b n) k"))
+
+        dummy = keep.tile([P, 1], F32, name="dummy")
+        nc.vector.memset(dummy[:], 0.0)
+        wsc = [keep.tile([P, 2, H], U8, name="wsc%d" % w, align_bytes=64) for w in range(2)]
+        for w in range(2):
+            nc.vector.memset(wsc[w][:].bitcast(I32), 0)
+        rows = keep.tile([P, P], BF16, name="rows")
+        nc.vector.memset(rows[:], 0.0)
+        w2s = keep.tile([P, 2, F], U8, name="w2s", align_bytes=64)
+        nc.vector.memset(w2s[:].bitcast(I32), 0)
+        stile = keep.tile([P, P], F32, name="stile")
+        nc.vector.memset(stile[:], 0.0)
+
+        ident = keep.tile([P, P], F32, name="ident")
+        make_identity(nc, ident[:])
+
+        w_words = [wa_words, wb_words]
+        w_scales = [wa_scales, wb_scales]
+        wt = [[keep.tile([P, 2, 512], U32, name="w%d_%d" % (w, gh), align_bytes=64) for gh in range(2)] for w in range(2)]
+
+        def load_w(w, gh):
+            nc.sync.dma_start(
+                out=wt[w][gh][:].bitcast(I32),
+                in_=w_words[w].bitcast(I32).rearrange("g p n o -> p g (n o)")[:, :, gh * 512 : gh * 512 + 512],
+            )
+
+        def load_scales(queue, dst, src, k):
+            for r in range(4):
+                queue.dma_start(
+                    out=dst[k + r : P : 32, :, :].bitcast(I32),
+                    in_=src.bitcast(I32)[:, r:16:4, :].rearrange("g q n -> q g n"),
+                )
+
+        dummy2 = keep.tile([P, 1], F32, name="dummy2")
+        nc.scalar.activation(out=dummy2[:], in_=dummy[:], func=ACT.Relu)
+        load_scales(nc.sync, wsc[0], wa_scales, 0)
+        load_w(0, 0)
+        load_w(1, 0)
+        load_scales(nc.sync, wsc[1], wb_scales, 0)
+        load_w(0, 1)
+        load_w(1, 1)
+        w2t = keep.tile([P, 2, F], U32, name="w2t", align_bytes=64)
+        nc.sync.dma_start(out=w2t[:].bitcast(I32), in_=w2_words.bitcast(I32).rearrange("g p n o -> p g (n o)"))
+        cs = keep.tile([P, 2, 4], BF16, name="cs")
+        nc.gpsimd.dma_start(out=cs[:], in_=c.rearrange("(g p t) -> p g t", g=2, t=4))
+        nc.gpsimd.dma_start(out=rows[0:4, :], in_=b2.rearrange("(c p) -> c p", p=P))
+        nc.gpsimd.dma_start(out=rows[4:8, :], in_=v.rearrange("(c p) -> c p", p=P))
+        load_scales(nc.gpsimd, w2s, w2_scales, 0)
+
+        xw = keep.tile([P, D], BF16, name="xw", align_bytes=64)
+        xg = keep.tile([P, 2, P, 4], BF16, name="xg", align_bytes=64)
+        xc = keep.tile([P, 2, P], U32, name="xc", align_bytes=64)
+        xq = keep.tile([P, 2, P], U8, name="xq", align_bytes=64)
+        xt = bank("m", [P, 2, 2, P], F32, "xt", 3)
+        for g in range(2):
+            for q in range(4 * g, 4 * g + 4):
+                src = xb[:, q * P : q * P + P].bitcast(FP8)
+                dst = xw[:, q * P : q * P + P]
+                if q % 2 == 0:
+                    nc.vector.tensor_scalar(out=dst, in0=src, scalar1=xs[:, q : q + 1], scalar2=None, op0=ALU.mult)
+                else:
+                    nc.scalar.activation(out=dst, in_=src, func=ACT.Copy, scale=xs[:, q : q + 1])
+        xwords = xw[:].bitcast(F32)
+        for g in range(2):
+            for u in range(2):
+                nc.tensor.transpose(xt[:, g, u, :], xwords[:, 256 * g + u : 256 * g + 256 : 2], ident[:])
+        nc.vector.tensor_copy(out=xg[:, 0].bitcast(F32), in_=xt[:, 0].rearrange("p u r -> p r u"))
+        nc.scalar.copy(out=xg[:, 1].bitcast(F32), in_=xt[:, 1].rearrange("p u r -> p r u"))
+        ident_b = keep.tile([P, P], BF16, name="ident_b")
+        nc.vector.tensor_copy(out=ident_b[:], in_=ident[:])
+        for g in range(2):
+            nc.vector.quantize_mx(
+                out=xc[:, g, :].bitcast(FP8X4), scales=xq[:, g, :], in_=xg[:, g].rearrange("p r t -> p (r t)")
+            )
+
+        a_sb = [[keep.tile([P, 4, P], F32, name="tok%d_%d" % (w, gh)) for gh in range(2)] for w in range(2)]
+        hid = [[keep.tile([P, P, 4], F32, name="hid%d_%d" % (w, gh)) for gh in range(2)] for w in range(2)]
+
+        gsrc = {}
+        ident_t = ident[:].rearrange("p (b i) -> p i b", b=B)
+
+        def keep_g(gh):
+            nc.scalar.copy(out=hid[1][gh][:], in_=gsrc.pop(gh))
+
+        def first(gh):
+            outs = []
+            for w in range(2):
+                o = bank("m", [P, 512], F32, "first%d_%d" % (w, gh), 3)
+                for g in range(2):
+                    nc.tensor.matmul_mx(
+                        out=o[:],
+                        lhsT=xc[:, g, :].bitcast(FP8X4),
+                        lhsT_scale=xq[:, g, :],
+                        rhs=wt[w][gh][:, g, :].bitcast(FP8X4),
+                        rhs_scale=wsc[w][:, g, gh * 512 : gh * 512 + 512],
+                        start=g == 0,
+                        stop=g == 1,
+                    )
+                outs.append(o)
+            for w in range(2):
+                src = outs[w][:].rearrange("p (m t) -> p t m", t=4)
+                if w == 1 and gh == 0:
+                    nc.vector.tensor_copy(out=a_sb[w][gh][:], in_=src)
+                else:
+                    nc.scalar.copy(out=a_sb[w][gh][:], in_=src)
+            tr = []
+            for w in range(2):
+                o = bank("acc%d" % (2 * gh + w), [P, 4, P], F32, "turn%d_%d" % (w, gh))
+                for t in range(4):
+                    nc.tensor.transpose(o[:, t, :], a_sb[w][gh][:, t, :], ident_t if w == 1 else ident[:])
+                tr.append(o)
+            for w in range(2):
+                src = tr[w][:].rearrange("p t k -> p k t")
+                if w == 0:
+                    nc.vector.tensor_tensor(
+                        out=hid[w][gh][:], in0=src, in1=cs[:, gh, :].unsqueeze(1).to_broadcast([P, P, 4]), op=ALU.add
+                    )
+                else:
+                    gsrc[gh] = src
+
+        b2c = keep.tile([P, 4], F32, name="b2c")
+        b2i = keep.tile([P, 4], F32, name="b2i")
+        vc = keep.tile([P, 4], BF16, name="vc")
+        vb = keep.tile([P, F], BF16, name="vb")
+
+        first(0)
+        ct = bank("lin", [P, P], BF16, "ct")
+        nc.tensor.transpose(ct[:], rows[:], ident_b[:])
+        nc.scalar.copy(out=vc[:], in_=ct[:, 4:8])
+        nc.scalar.copy(out=b2c[:], in_=ct[:, 0:4])
+        nc.scalar.activation(out=b2i[:], in_=ct[:, 0:4], func=ACT.Copy, scale=16.0 / 3.0)
+
+        units = [(ci, gh) for ci in range(len(CHUNKS)) for gh in range(2)]
+        ys, ss, zs, zc, zq, rr = {}, {}, {}, {}, {}, {}
+        acc, lin = [], []
+
+        def pair_add(k):
+            ci, gh = units[k]
+            j0, jn = CHUNKS[ci]
+            y = work.tile([P, 2048], BF16, tag="y", name="y%d" % k, bufs=4, align_bytes=64)
+            ys[k] = y
+            g = gsrc.get(gh, hid[1][gh][:])
+            nc.vector.tensor_tensor(
+                out=y[:, : jn * 512].rearrange("p (j b i t) -> p j b i t", j=jn, b=B, t=4),
+                in0=hid[0][gh][:]
+                .rearrange("p (b i) t -> p b i t", b=B)
+                .unsqueeze(1)
+                .to_broadcast([P, jn, B, N, 4]),
+                in1=g.rearrange("p (j b) t -> p j b t", b=B)[:, j0 : j0 + jn]
+                .unsqueeze(3)
+                .to_broadcast([P, jn, B, N, 4]),
+                op=ALU.add,
+            )
+
+        def quarter(k):
+            w = CHUNKS[units[k][0]][1] * 512
+            s = work.tile([P, 2048], BF16, tag="s", name="s%d" % k, bufs=3, align_bytes=64)
+            ss[k] = s
+            if k in QV:
+                nc.vector.tensor_scalar(out=s[:, :w], in0=ys[k][:, :w], scalar1=0.25, scalar2=None, op0=ALU.mult)
+            else:
+                nc.scalar.activation(out=s[:, :w], in_=ys[k][:, :w], func=ACT.Copy, scale=0.25)
+
+        def leaky(k):
+            w = CHUNKS[units[k][0]][1] * 512
+            z = work.tile([P, 2048], BF16, tag="z", name="z%d" % k, bufs=3, align_bytes=64)
+            zs[k] = z
+            nc.vector.tensor_tensor(out=z[:, :w], in0=ys[k][:, :w], in1=ss[k][:, :w], op=ALU.max)
+
+        def quant(k):
+            n = CHUNKS[units[k][0]][1] * P
+            zc[k] = work.tile([P, 512], U32, tag="zc", name="zc%d" % k, bufs=5, align_bytes=64)
+            zq[k] = work.tile([P, 512], U8, tag="zq", name="zq%d" % k, bufs=5, align_bytes=64)
+            nc.vector.quantize_mx(out=zc[k][:, :n].bitcast(FP8X4), scales=zq[k][:, :n], in_=zs[k][:, : 4 * n])
+
+        banks = {}
+
+        def main_mm(ci, fc, gh):
+            n = CHUNKS[ci][1] * P
+            if gh == 0:
+                banks[ci, fc] = bank("m", [P, 512], F32, "main%d_%d" % (ci, fc), 3)
+            k = 2 * ci + gh
+            nc.tensor.matmul_mx(
+                out=banks[ci, fc][:, :n],
+                lhsT=w2t[:, gh, fc * P : fc * P + P].bitcast(FP8X4),
+                lhsT_scale=w2s[:, gh, fc * P : fc * P + P],
+                rhs=zc[k][:, :n].bitcast(FP8X4),
+                rhs_scale=zq[k][:, :n],
+                start=gh == 0,
+                stop=gh == 1,
+            )
+
+        def lin_mm(ci, gh):
+            jn = CHUNKS[ci][1]
+            k = 2 * ci + gh
+            for j in range(jn):
+                nc.tensor.matmul_mx(
+                    out=lin[0][:],
+                    lhsT=zc[k][:, j * P : j * P + P].bitcast(FP8X4),
+                    lhsT_scale=zq[k][:, j * P : j * P + P],
+                    rhs=w2t[:, gh, :].bitcast(FP8X4),
+                    rhs_scale=w2s[:, gh, :],
+                    start=ci == 0 and j == 0 and gh == 0,
+                    stop=ci == len(CHUNKS) - 1 and j == jn - 1 and gh == 1,
+                )
+
+        def relu(ci, fc, engine="scalar"):
+            n = CHUNKS[ci][1] * P
+            r = work.tile([P, 512], F32, tag="r", name="r%d_%d" % (ci, fc), bufs=8)
+            rr[ci, fc] = r
+            if engine == "scalar":
+                nc.scalar.activation(out=r[:, :n], in_=banks[ci, fc][:, :n], func=ACT.Relu, bias=b2c[:, fc : fc + 1])
+            else:
+                nc.vector.tensor_scalar(
+                    out=r[:, :n],
+                    in0=banks[ci, fc][:, :n],
+                    scalar1=b2c[:, fc : fc + 1],
+                    scalar2=0.0,
+                    op0=ALU.add,
+                    op1=ALU.max,
+                )
+
+        def pool(ci, fc):
+            jn = CHUNKS[ci][1]
+            for j in range(jn):
+                nc.tensor.matmul(
+                    acc[fc][:],
+                    rr[ci, fc][:, j * P : j * P + P],
+                    ident[:],
+                    is_transpose=True,
+                    start=False,
+                    stop=ci == len(CHUNKS) - 1 and j == jn - 1,
+                )
+
+        def open_sums():
+            for fc in range(4):
+                o = bank("acc%d" % fc, [P, P], F32, "pool%d" % fc)
+                acc.append(o)
+                nc.tensor.matmul(
+                    o[:], b2i[:, fc : fc + 1].to_broadcast([P, P]), ident[:], is_transpose=True, start=True, stop=False
+                )
+            lin.append(bank("lin", [P, F], F32, "lin"))
+
+        last = len(units)
+        nch = len(CHUNKS)
+        for k in range(last + 2):
+            if k < last:
+                pair_add(k)
+                if k in QV:
+                    quarter(k)
+            if k == 0:
+                first(1)
+            q = k - 2
+            if 0 <= q < last:
+                quant(q)
+            if 0 <= k - 1 < last:
+                leaky(k - 1)
+            if k == 2:
+                open_sums()
+            if k < last and k not in QV:
+                quarter(k)
+            if k < 2:
+                keep_g(k)
+            if k == 2:
+                vt = bank("m", [P, F], BF16, "vt", 3)
+                for fc in range(4):
+                    nc.tensor.transpose(vt[:, fc * P : fc * P + P], vc[:, fc : fc + 1].to_broadcast([P, P]), ident_b[:])
+                nc.scalar.copy(out=vb[:], in_=vt[:])
+            if 0 <= q < last:
+                ci, gh = units[q]
+                if gh == 0:
+                    lin_mm(ci, 0)
+                    for fc in range(3):
+                        main_mm(ci, fc, 0)
+                elif ci < nch - 1:
+                    for fc in range(3):
+                        main_mm(ci, fc, 1)
+                        relu(ci, fc)
+                    lin_mm(ci, 1)
+                    main_mm(ci, 3, 0)
+                    main_mm(ci, 3, 1)
+                    relu(ci, 3)
+                    if ci > 0:
+                        for fc in range(4):
+                            pool(ci - 1, fc)
+
+        ci = nch - 1
+        lins = keep.tile([P, F], F32, name="lins")
+        for fc in range(4):
+            pool(ci - 1, fc)
+        for fc in range(3):
+            main_mm(ci, fc, 1)
+        relu(ci, 0, "vector")
+        relu(ci, 1)
+        relu(ci, 2, "vector")
+        lin_mm(ci, 1)
+        main_mm(ci, 3, 0)
+        main_mm(ci, 3, 1)
+        nc.scalar.activation(out=lins[:], in_=lin[0][:], func=ACT.Copy, scale=1.0 / 64.0)
+        relu(ci, 3, "vector")
+        for fc in range(4):
+            pool(ci, fc)
+        pooled = keep.tile([P, F], F32, name="pooled")
+        for fc in range(4):
+            nc.vector.scalar_tensor_tensor(
+                out=pooled[:, fc * P : fc * P + P],
+                in0=acc[fc][:],
+                scalar=3.0 / 64.0,
+                in1=lins[:, fc * P : fc * P + P],
+                op0=ALU.mult,
+                op1=ALU.add,
+            )
+            if fc % 2 == 1:
+                f0 = fc * P - P
+                (nc.sync if fc == 1 else nc.scalar).dma_start(
+                    out=out_0.rearrange("b i f -> (b i) f")[:, f0 : f0 + 256], in_=pooled[:, f0 : f0 + 256]
+                )
+        prod = keep.tile([P, F], F32, name="prod")
+        nc.vector.scalar_tensor_tensor(
+            out=prod[:], in0=pooled[:], scalar=1.0, in1=vb[:], op0=ALU.mult, op1=ALU.mult, accum_out=stile[:, 0:1]
+        )
+        st = bank("m", [P, P], F32, "st", 3)
+        nc.tensor.transpose(st[:], stile[:], ident[:])
+        srow = keep.tile([1, P], F32, name="srow")
+        nc.vector.tensor_copy(out=srow[:], in_=st[0:1, :])
+        nc.sync.dma_start(out=out_1.rearrange("(o b) i -> o (b i)", o=1), in_=srow[:])

@@ -4,8 +4,7 @@ import concourse.mybir as mybir
 from concourse.masks import make_identity
 
 B, N, D, H, F = 8, 16, 1024, 1024, 512
-T = B * N
-FLOPS = 2 * T * D * H * 2 + 2 * B * N * N * H * F
+FLOPS = 2 * (B * N) * D * H * 2 + 2 * (B * N * N) * H * F
 
 F32 = mybir.dt.float32
 BF16 = mybir.dt.bfloat16
@@ -18,8 +17,14 @@ ALU = mybir.AluOpType
 ACT = mybir.ActivationFunctionType
 
 P = 128
-CHUNKS = [(0, 4), (4, 4), (8, 2), (10, 2), (12, 2), (14, 1), (15, 1)]
-QV = [12, 13]
+T = 4
+PASS = P * T
+BLOCK = 128
+FCHUNKS = F // P
+
+CHUNKS = ((0, 4), (4, 4), (8, 2), (10, 2), (12, 2), (14, 2))
+LAST = len(CHUNKS) - 1
+UNIT = 4 * P * T
 
 
 def tile_groupwisepairrankingscorer_d1p_kernel(
@@ -32,336 +37,332 @@ def tile_groupwisepairrankingscorer_d1p_kernel(
         psum = ctx.enter_context(tc.psum_pool(name="psum", bufs=1))
         ctx.enter_context(tc.manual_schedule())
 
-        def bank(tag, shape, dtype, name, bufs=1):
-            return psum.tile(shape, dtype, tag=tag, name=name, bufs=bufs)
+        def rotating(shape, dtype, name):
+            return psum.tile(shape, dtype, tag="m", name=name, bufs=3)
 
-        xs = keep.tile([P, 8], F32, name="xs")
-        xb = keep.tile([P, D], U8, name="xb", align_bytes=64)
-        nc.sync.dma_start(out=xs[:], in_=x_scale.rearrange("b n q -> (b n) q"))
-        nc.sync.dma_start(out=xb[:], in_=x_bytes.rearrange("b n k -> (b n) k"))
+        def fixed(tag, shape, dtype, name):
+            return psum.tile(shape, dtype, tag=tag, name=name, bufs=1)
 
-        dummy = keep.tile([P, 1], F32, name="dummy")
-        nc.vector.memset(dummy[:], 0.0)
-        wsc = [keep.tile([P, 2, H], U8, name="wsc%d" % w, align_bytes=64) for w in range(2)]
-        for w in range(2):
-            nc.vector.memset(wsc[w][:].bitcast(I32), 0)
+        x_codes8 = keep.tile([P, D], U8, name="x_codes8", align_bytes=64)
+        x_scales = keep.tile([P, D // BLOCK], F32, name="x_scales")
+        nc.sync.dma_start(out=x_scales[:], in_=x_scale.rearrange("b n q -> (b n) q"))
+        nc.sync.dma_start(out=x_codes8[:], in_=x_bytes.rearrange("b n k -> (b n) k"))
+
         rows = keep.tile([P, P], BF16, name="rows")
         nc.vector.memset(rows[:], 0.0)
-        w2s = keep.tile([P, 2, F], U8, name="w2s", align_bytes=64)
-        nc.vector.memset(w2s[:].bitcast(I32), 0)
-        stile = keep.tile([P, P], F32, name="stile")
-        nc.vector.memset(stile[:], 0.0)
+        score_cols = keep.tile([P, P], F32, name="score_cols")
+        nc.scalar.activation(out=score_cols[:], in_=rows[:], func=ACT.Relu)
+        w1_scales = [keep.tile([P, 2, H], U8, name="w1_scales%d" % w, align_bytes=64) for w in range(2)]
+        for w in range(2):
+            nc.vector.memset(w1_scales[w][:].bitcast(I32), 0)
+        w2_scale = keep.tile([P, 2, F], U8, name="w2_scale", align_bytes=64)
+        nc.vector.memset(w2_scale[:].bitcast(I32), 0)
 
         ident = keep.tile([P, P], F32, name="ident")
         make_identity(nc, ident[:])
 
-        w_words = [wa_words, wb_words]
-        w_scales = [wa_scales, wb_scales]
-        wt = [[keep.tile([P, 2, 512], U32, name="w%d_%d" % (w, gh), align_bytes=64) for gh in range(2)] for w in range(2)]
+        w1_codes = [
+            [keep.tile([P, 2, PASS], U32, name="w1_codes%d_%d" % (w, half), align_bytes=64) for half in range(2)]
+            for w in range(2)
+        ]
 
-        def load_w(w, gh):
+        def load_w1(words, w, half):
             nc.sync.dma_start(
-                out=wt[w][gh][:].bitcast(I32),
-                in_=w_words[w].bitcast(I32).rearrange("g p n o -> p g (n o)")[:, :, gh * 512 : gh * 512 + 512],
+                out=w1_codes[w][half][:].bitcast(I32),
+                in_=words.bitcast(I32).rearrange("g p n o -> p g (n o)")[:, :, half * PASS : half * PASS + PASS],
             )
 
-        def load_scales(queue, dst, src, k):
+        def load_scales(queue, dst, src):
             for r in range(4):
                 queue.dma_start(
-                    out=dst[k + r : P : 32, :, :].bitcast(I32),
+                    out=dst[r:P:32, :, :].bitcast(I32),
                     in_=src.bitcast(I32)[:, r:16:4, :].rearrange("g q n -> q g n"),
                 )
 
-        dummy2 = keep.tile([P, 1], F32, name="dummy2")
-        nc.scalar.activation(out=dummy2[:], in_=dummy[:], func=ACT.Relu)
-        load_scales(nc.sync, wsc[0], wa_scales, 0)
-        load_w(0, 0)
-        load_w(1, 0)
-        load_scales(nc.sync, wsc[1], wb_scales, 0)
-        load_w(0, 1)
-        load_w(1, 1)
-        w2t = keep.tile([P, 2, F], U32, name="w2t", align_bytes=64)
-        nc.sync.dma_start(out=w2t[:].bitcast(I32), in_=w2_words.bitcast(I32).rearrange("g p n o -> p g (n o)"))
-        cs = keep.tile([P, 2, 4], BF16, name="cs")
-        nc.gpsimd.dma_start(out=cs[:], in_=c.rearrange("(g p t) -> p g t", g=2, t=4))
-        nc.gpsimd.dma_start(out=rows[0:4, :], in_=b2.rearrange("(c p) -> c p", p=P))
-        nc.gpsimd.dma_start(out=rows[4:8, :], in_=v.rearrange("(c p) -> c p", p=P))
-        load_scales(nc.gpsimd, w2s, w2_scales, 0)
+        load_scales(nc.sync, w1_scales[0], wa_scales)
+        load_w1(wa_words, 0, 0)
+        load_w1(wb_words, 1, 0)
+        load_scales(nc.sync, w1_scales[1], wb_scales)
+        load_w1(wa_words, 0, 1)
+        load_w1(wb_words, 1, 1)
+        w2_codes = keep.tile([P, 2, F], U32, name="w2_codes", align_bytes=64)
+        nc.sync.dma_start(out=w2_codes[:].bitcast(I32), in_=w2_words.bitcast(I32).rearrange("g p n o -> p g (n o)"))
+        c_cols = keep.tile([P, 2, T], BF16, name="c_cols")
+        nc.gpsimd.dma_start(out=c_cols[:], in_=c.rearrange("(g p t) -> p g t", g=2, t=T))
+        nc.gpsimd.dma_start(out=rows[0:FCHUNKS, :], in_=b2.rearrange("(c p) -> c p", p=P))
+        nc.gpsimd.dma_start(out=rows[FCHUNKS : 2 * FCHUNKS, :], in_=v.rearrange("(c p) -> c p", p=P))
+        load_scales(nc.gpsimd, w2_scale, w2_scales)
 
-        xw = keep.tile([P, D], BF16, name="xw", align_bytes=64)
-        xg = keep.tile([P, 2, P, 4], BF16, name="xg", align_bytes=64)
-        xc = keep.tile([P, 2, P], U32, name="xc", align_bytes=64)
-        xq = keep.tile([P, 2, P], U8, name="xq", align_bytes=64)
-        xt = bank("m", [P, 2, 2, P], F32, "xt", 3)
-        for g in range(2):
-            for q in range(4 * g, 4 * g + 4):
-                src = xb[:, q * P : q * P + P].bitcast(FP8)
-                dst = xw[:, q * P : q * P + P]
-                if q % 2 == 0:
-                    nc.vector.tensor_scalar(out=dst, in0=src, scalar1=xs[:, q : q + 1], scalar2=None, op0=ALU.mult)
-                else:
-                    nc.scalar.activation(out=dst, in_=src, func=ACT.Copy, scale=xs[:, q : q + 1])
-        xwords = xw[:].bitcast(F32)
+        x_wide = keep.tile([P, D], BF16, name="x_wide", align_bytes=64)
+        for q in range(D // BLOCK):
+            cols = slice(q * BLOCK, q * BLOCK + BLOCK)
+            src = x_codes8[:, cols].bitcast(FP8)
+            scale = x_scales[:, q : q + 1]
+            if q % 2 == 0:
+                nc.vector.tensor_scalar(out=x_wide[:, cols], in0=src, scalar1=scale, scalar2=None, op0=ALU.mult)
+            else:
+                nc.scalar.activation(out=x_wide[:, cols], in_=src, func=ACT.Copy, scale=scale)
+
+        x_words = x_wide[:].bitcast(F32)
+        x_turned = [rotating([P, 2, P], F32, "x_turned%d" % g) for g in range(2)]
         for g in range(2):
             for u in range(2):
-                nc.tensor.transpose(xt[:, g, u, :], xwords[:, 256 * g + u : 256 * g + 256 : 2], ident[:])
-        nc.vector.tensor_copy(out=xg[:, 0].bitcast(F32), in_=xt[:, 0].rearrange("p u r -> p r u"))
-        nc.scalar.copy(out=xg[:, 1].bitcast(F32), in_=xt[:, 1].rearrange("p u r -> p r u"))
-        ident_b = keep.tile([P, P], BF16, name="ident_b")
-        nc.vector.tensor_copy(out=ident_b[:], in_=ident[:])
+                nc.tensor.transpose(x_turned[g][:, u, :], x_words[:, 256 * g + u : 256 * g + 256 : 2], ident[:])
+        x_grouped = keep.tile([P, 2, P, T], BF16, name="x_grouped", align_bytes=64)
+        nc.vector.tensor_copy(out=x_grouped[:, 0].bitcast(F32), in_=x_turned[0][:].rearrange("p u d -> p d u"))
+        nc.scalar.copy(out=x_grouped[:, 1].bitcast(F32), in_=x_turned[1][:].rearrange("p u d -> p d u"))
+        ident_bf = keep.tile([P, P], BF16, name="ident_bf")
+        nc.vector.tensor_copy(out=ident_bf[:], in_=ident[:])
+        x_codes = keep.tile([P, 2, P], U32, name="x_codes", align_bytes=64)
+        x_mx_scales = keep.tile([P, 2, P], U8, name="x_mx_scales", align_bytes=64)
         for g in range(2):
             nc.vector.quantize_mx(
-                out=xc[:, g, :].bitcast(FP8X4), scales=xq[:, g, :], in_=xg[:, g].rearrange("p r t -> p (r t)")
+                out=x_codes[:, g, :].bitcast(FP8X4),
+                scales=x_mx_scales[:, g, :],
+                in_=x_grouped[:, g].rearrange("p d t -> p (d t)"),
             )
 
-        a_sb = [[keep.tile([P, 4, P], F32, name="tok%d_%d" % (w, gh)) for gh in range(2)] for w in range(2)]
-        hid = [[keep.tile([P, P, 4], F32, name="hid%d_%d" % (w, gh)) for gh in range(2)] for w in range(2)]
+        by_doc = [[keep.tile([P, T, P], F32, name="by_doc%d_%d" % (w, half)) for half in range(2)] for w in range(2)]
+        a_c = [keep.tile([P, P, T], F32, name="a_c%d" % half) for half in range(2)]
+        g_kept = [keep.tile([P, P, T], F32, name="g_kept%d" % half) for half in range(2)]
+        g_psum = {}
+        ident_jb = ident[:].rearrange("p (b j) -> p j b", b=B)
 
-        gsrc = {}
-        ident_t = ident[:].rearrange("p (b i) -> p i b", b=B)
-
-        def keep_g(gh):
-            nc.scalar.copy(out=hid[1][gh][:], in_=gsrc.pop(gh))
-
-        def first(gh):
-            outs = []
+        def first_products(half):
+            banks = []
             for w in range(2):
-                o = bank("m", [P, 512], F32, "first%d_%d" % (w, gh), 3)
+                o = rotating([P, PASS], F32, "first%d_%d" % (w, half))
                 for g in range(2):
                     nc.tensor.matmul_mx(
                         out=o[:],
-                        lhsT=xc[:, g, :].bitcast(FP8X4),
-                        lhsT_scale=xq[:, g, :],
-                        rhs=wt[w][gh][:, g, :].bitcast(FP8X4),
-                        rhs_scale=wsc[w][:, g, gh * 512 : gh * 512 + 512],
+                        lhsT=x_codes[:, g, :].bitcast(FP8X4),
+                        lhsT_scale=x_mx_scales[:, g, :],
+                        rhs=w1_codes[w][half][:, g, :].bitcast(FP8X4),
+                        rhs_scale=w1_scales[w][:, g, half * PASS : half * PASS + PASS],
                         start=g == 0,
                         stop=g == 1,
                     )
-                outs.append(o)
+                banks.append(o)
             for w in range(2):
-                src = outs[w][:].rearrange("p (m t) -> p t m", t=4)
-                if w == 1 and gh == 0:
-                    nc.vector.tensor_copy(out=a_sb[w][gh][:], in_=src)
-                else:
-                    nc.scalar.copy(out=a_sb[w][gh][:], in_=src)
-            tr = []
+                nc.scalar.copy(out=by_doc[w][half][:], in_=banks[w][:].rearrange("p (m t) -> p t m", t=T))
+            turned = []
             for w in range(2):
-                o = bank("acc%d" % (2 * gh + w), [P, 4, P], F32, "turn%d_%d" % (w, gh))
-                for t in range(4):
-                    nc.tensor.transpose(o[:, t, :], a_sb[w][gh][:, t, :], ident_t if w == 1 else ident[:])
-                tr.append(o)
-            for w in range(2):
-                src = tr[w][:].rearrange("p t k -> p k t")
-                if w == 0:
-                    nc.vector.tensor_tensor(
-                        out=hid[w][gh][:], in0=src, in1=cs[:, gh, :].unsqueeze(1).to_broadcast([P, P, 4]), op=ALU.add
-                    )
-                else:
-                    gsrc[gh] = src
-
-        b2c = keep.tile([P, 4], F32, name="b2c")
-        b2i = keep.tile([P, 4], F32, name="b2i")
-        vc = keep.tile([P, 4], BF16, name="vc")
-        vb = keep.tile([P, F], BF16, name="vb")
-
-        first(0)
-        ct = bank("lin", [P, P], BF16, "ct")
-        nc.tensor.transpose(ct[:], rows[:], ident_b[:])
-        nc.scalar.copy(out=vc[:], in_=ct[:, 4:8])
-        nc.scalar.copy(out=b2c[:], in_=ct[:, 0:4])
-        nc.scalar.activation(out=b2i[:], in_=ct[:, 0:4], func=ACT.Copy, scale=16.0 / 3.0)
-
-        units = [(ci, gh) for ci in range(len(CHUNKS)) for gh in range(2)]
-        ys, ss, zs, zc, zq, rr = {}, {}, {}, {}, {}, {}
-        acc, lin = [], []
-
-        def pair_add(k):
-            ci, gh = units[k]
-            j0, jn = CHUNKS[ci]
-            y = work.tile([P, 2048], BF16, tag="y", name="y%d" % k, bufs=4, align_bytes=64)
-            ys[k] = y
-            g = gsrc.get(gh, hid[1][gh][:])
+                o = fixed("acc%d" % (2 * half + w), [P, T, P], F32, "turned%d_%d" % (w, half))
+                for t in range(T):
+                    nc.tensor.transpose(o[:, t, :], by_doc[w][half][:, t, :], ident_jb if w == 1 else ident[:])
+                turned.append(o[:].rearrange("p t d -> p d t"))
             nc.vector.tensor_tensor(
-                out=y[:, : jn * 512].rearrange("p (j b i t) -> p j b i t", j=jn, b=B, t=4),
-                in0=hid[0][gh][:]
+                out=a_c[half][:], in0=turned[0], in1=c_cols[:, half, :].unsqueeze(1).to_broadcast([P, P, T]), op=ALU.add
+            )
+            g_psum[half] = turned[1]
+
+        first_products(0)
+
+        columns = fixed("lin", [P, P], BF16, "columns")
+        nc.tensor.transpose(columns[:], rows[:], ident_bf[:])
+
+        units = [(ci, half) for ci in range(len(CHUNKS)) for half in range(2)]
+        ys, quarters, zs, codes, products_of, relus = {}, {}, {}, {}, {}, {}
+
+        def width(k):
+            return CHUNKS[units[k][0]][1] * P * T
+
+        def add_pairs(k):
+            ci, half = units[k]
+            j0, jn = CHUNKS[ci]
+            ys[k] = work.tile([P, UNIT], BF16, tag="y", name="y%d" % k, bufs=4, align_bytes=64)
+            g = g_psum.get(half, g_kept[half][:])
+            nc.vector.tensor_tensor(
+                out=ys[k][:, : width(k)].rearrange("p (j b i t) -> p j b i t", j=jn, b=B, t=T),
+                in0=a_c[half][:]
                 .rearrange("p (b i) t -> p b i t", b=B)
                 .unsqueeze(1)
-                .to_broadcast([P, jn, B, N, 4]),
+                .to_broadcast([P, jn, B, N, T]),
                 in1=g.rearrange("p (j b) t -> p j b t", b=B)[:, j0 : j0 + jn]
                 .unsqueeze(3)
-                .to_broadcast([P, jn, B, N, 4]),
+                .to_broadcast([P, jn, B, N, T]),
                 op=ALU.add,
             )
 
+        def keep_g(half):
+            nc.scalar.copy(out=g_kept[half][:], in_=g_psum.pop(half))
+
         def quarter(k):
-            w = CHUNKS[units[k][0]][1] * 512
-            s = work.tile([P, 2048], BF16, tag="s", name="s%d" % k, bufs=3, align_bytes=64)
-            ss[k] = s
-            if k in QV:
-                nc.vector.tensor_scalar(out=s[:, :w], in0=ys[k][:, :w], scalar1=0.25, scalar2=None, op0=ALU.mult)
+            quarters[k] = work.tile([P, UNIT], BF16, tag="quarter", name="quarter%d" % k, bufs=3, align_bytes=64)
+            out, src = quarters[k][:, : width(k)], ys[k][:, : width(k)]
+            if k == len(units) - 1:
+                nc.vector.tensor_scalar(out=out, in0=src, scalar1=0.25, scalar2=None, op0=ALU.mult)
             else:
-                nc.scalar.activation(out=s[:, :w], in_=ys[k][:, :w], func=ACT.Copy, scale=0.25)
+                nc.scalar.activation(out=out, in_=src, func=ACT.Copy, scale=0.25)
 
         def leaky(k):
-            w = CHUNKS[units[k][0]][1] * 512
-            z = work.tile([P, 2048], BF16, tag="z", name="z%d" % k, bufs=3, align_bytes=64)
-            zs[k] = z
-            nc.vector.tensor_tensor(out=z[:, :w], in0=ys[k][:, :w], in1=ss[k][:, :w], op=ALU.max)
+            w = width(k)
+            zs[k] = work.tile([P, UNIT], BF16, tag="z", name="z%d" % k, bufs=3, align_bytes=64)
+            nc.vector.tensor_tensor(out=zs[k][:, :w], in0=ys[k][:, :w], in1=quarters[k][:, :w], op=ALU.max)
 
-        def quant(k):
-            n = CHUNKS[units[k][0]][1] * P
-            zc[k] = work.tile([P, 512], U32, tag="zc", name="zc%d" % k, bufs=5, align_bytes=64)
-            zq[k] = work.tile([P, 512], U8, tag="zq", name="zq%d" % k, bufs=5, align_bytes=64)
-            nc.vector.quantize_mx(out=zc[k][:, :n].bitcast(FP8X4), scales=zq[k][:, :n], in_=zs[k][:, : 4 * n])
-
-        banks = {}
-
-        def main_mm(ci, fc, gh):
-            n = CHUNKS[ci][1] * P
-            if gh == 0:
-                banks[ci, fc] = bank("m", [P, 512], F32, "main%d_%d" % (ci, fc), 3)
-            k = 2 * ci + gh
-            nc.tensor.matmul_mx(
-                out=banks[ci, fc][:, :n],
-                lhsT=w2t[:, gh, fc * P : fc * P + P].bitcast(FP8X4),
-                lhsT_scale=w2s[:, gh, fc * P : fc * P + P],
-                rhs=zc[k][:, :n].bitcast(FP8X4),
-                rhs_scale=zq[k][:, :n],
-                start=gh == 0,
-                stop=gh == 1,
+        def quantise(k):
+            n = width(k) // T
+            words = work.tile([P, UNIT // T], U32, tag="z_words", name="z_words%d" % k, bufs=5, align_bytes=64)
+            scales = work.tile([P, UNIT // T], U8, tag="z_scales", name="z_scales%d" % k, bufs=5, align_bytes=64)
+            nc.vector.quantize_mx(
+                out=words[:, :n].bitcast(FP8X4), scales=scales[:, :n], in_=zs[k][:, : width(k)]
             )
+            codes[units[k]] = (words, scales)
 
-        def lin_mm(ci, gh):
-            jn = CHUNKS[ci][1]
-            k = 2 * ci + gh
-            for j in range(jn):
-                nc.tensor.matmul_mx(
-                    out=lin[0][:],
-                    lhsT=zc[k][:, j * P : j * P + P].bitcast(FP8X4),
-                    lhsT_scale=zq[k][:, j * P : j * P + P],
-                    rhs=w2t[:, gh, :].bitcast(FP8X4),
-                    rhs_scale=w2s[:, gh, :],
-                    start=ci == 0 and j == 0 and gh == 0,
-                    stop=ci == len(CHUNKS) - 1 and j == jn - 1 and gh == 1,
-                )
-
-        def relu(ci, fc, engine="scalar"):
-            n = CHUNKS[ci][1] * P
-            r = work.tile([P, 512], F32, tag="r", name="r%d_%d" % (ci, fc), bufs=8)
-            rr[ci, fc] = r
-            if engine == "scalar":
-                nc.scalar.activation(out=r[:, :n], in_=banks[ci, fc][:, :n], func=ACT.Relu, bias=b2c[:, fc : fc + 1])
-            else:
-                nc.vector.tensor_scalar(
-                    out=r[:, :n],
-                    in0=banks[ci, fc][:, :n],
-                    scalar1=b2c[:, fc : fc + 1],
-                    scalar2=0.0,
-                    op0=ALU.add,
-                    op1=ALU.max,
-                )
-
-        def pool(ci, fc):
-            jn = CHUNKS[ci][1]
-            for j in range(jn):
-                nc.tensor.matmul(
-                    acc[fc][:],
-                    rr[ci, fc][:, j * P : j * P + P],
-                    ident[:],
-                    is_transpose=True,
-                    start=False,
-                    stop=ci == len(CHUNKS) - 1 and j == jn - 1,
-                )
+        sums = []
+        lin = []
 
         def open_sums():
-            for fc in range(4):
-                o = bank("acc%d" % fc, [P, P], F32, "pool%d" % fc)
-                acc.append(o)
+            for fc in range(FCHUNKS):
+                sums.append(fixed("acc%d" % fc, [P, P], F32, "sum%d" % fc))
                 nc.tensor.matmul(
-                    o[:], b2i[:, fc : fc + 1].to_broadcast([P, P]), ident[:], is_transpose=True, start=True, stop=False
+                    sums[fc][:], b2_lin[:, fc : fc + 1].to_broadcast([P, P]), ident[:],
+                    is_transpose=True, start=True, stop=False,
                 )
-            lin.append(bank("lin", [P, F], F32, "lin"))
+            lin.append(fixed("lin", [P, F], F32, "lin"))
 
-        last = len(units)
-        nch = len(CHUNKS)
-        for k in range(last + 2):
-            if k < last:
-                pair_add(k)
-                if k in QV:
-                    quarter(k)
+        def product(ci, fc, half):
+            n = CHUNKS[ci][1] * P
+            if half == 0 and ci < LAST:
+                products_of[ci, fc] = rotating([P, PASS], F32, "product%d_%d" % (ci, fc))[:, :n]
+            elif half == 0 and fc % 2 == 0:
+                o = rotating([P, PASS], F32, "product%d_%d" % (ci, fc))
+                products_of[ci, fc], products_of[ci, fc + 1] = o[:, :n], o[:, n : 2 * n]
+            words, scales = codes[ci, half]
+            nc.tensor.matmul_mx(
+                out=products_of[ci, fc],
+                lhsT=w2_codes[:, half, fc * P : fc * P + P].bitcast(FP8X4),
+                lhsT_scale=w2_scale[:, half, fc * P : fc * P + P],
+                rhs=words[:, :n].bitcast(FP8X4),
+                rhs_scale=scales[:, :n],
+                start=half == 0,
+                stop=half == 1,
+            )
+
+        def linear(ci, half):
+            words, scales = codes[ci, half]
+            for j in range(CHUNKS[ci][1]):
+                cols = slice(j * P, j * P + P)
+                nc.tensor.matmul_mx(
+                    out=lin[0][:],
+                    lhsT=words[:, cols].bitcast(FP8X4),
+                    lhsT_scale=scales[:, cols],
+                    rhs=w2_codes[:, half, :].bitcast(FP8X4),
+                    rhs_scale=w2_scale[:, half, :],
+                    start=ci == 0 and j == 0 and half == 0,
+                    stop=ci == LAST - 1 and j == CHUNKS[ci][1] - 1 and half == 1,
+                )
+
+        def activate(ci, fc):
+            n = CHUNKS[ci][1] * P
+            r = work.tile([P, PASS], F32, tag="relu", name="relu%d_%d" % (ci, fc), bufs=16)
+            relus[ci, fc] = r
+            if ci < LAST:
+                nc.scalar.activation(
+                    out=r[:, :n], in_=products_of[ci, fc], func=ACT.Relu, scale=0.75, bias=b2_relu[:, fc : fc + 1]
+                )
+            else:
+                u = work.tile([P, PASS], F32, tag="u", name="u%d" % fc, bufs=4)
+                nc.scalar.activation(
+                    out=u[:, :n], in_=products_of[ci, fc], func=ACT.Identity, scale=0.25, bias=b2_quarter[:, fc : fc + 1]
+                )
+                nc.vector.scalar_tensor_tensor(
+                    out=r[:, :n], in0=u[:, :n], scalar=4.0, in1=u[:, :n], op0=ALU.mult, op1=ALU.max
+                )
+
+        def add_up(ci):
+            jn = CHUNKS[ci][1]
+            for fc in range(FCHUNKS):
+                for j in range(jn):
+                    nc.tensor.matmul(
+                        sums[fc][:], relus[ci, fc][:, j * P : j * P + P], ident[:],
+                        is_transpose=True, start=False, stop=ci == LAST and j == jn - 1,
+                    )
+
+        def second_stage(k):
+            ci, half = units[k]
+            if ci == LAST:
+                if half == 1:
+                    nc.scalar.activation(out=lin_mean[:], in_=lin[0][:], func=ACT.Copy, scale=0.25 / N)
+                    for f0 in (0, 2):
+                        for fc in (f0, f0 + 1):
+                            product(ci, fc, 0)
+                            product(ci, fc, 1)
+                        for fc in (f0, f0 + 1):
+                            activate(ci, fc)
+            elif half == 0:
+                linear(ci, 0)
+                for fc in range(3):
+                    product(ci, fc, 0)
+            else:
+                for fc in range(3):
+                    product(ci, fc, 1)
+                    activate(ci, fc)
+                linear(ci, 1)
+                product(ci, 3, 0)
+                product(ci, 3, 1)
+                activate(ci, 3)
+            if half == 1 and ci > 0:
+                add_up(ci - 1)
+
+        b2_relu = keep.tile([P, FCHUNKS], F32, name="b2_relu")
+        b2_quarter = keep.tile([P, FCHUNKS], F32, name="b2_quarter")
+        b2_lin = keep.tile([P, FCHUNKS], F32, name="b2_lin")
+        v_cols = keep.tile([P, FCHUNKS], BF16, name="v_cols")
+        v_all = keep.tile([P, F], BF16, name="v_all")
+        lin_mean = keep.tile([P, F], F32, name="lin_mean")
+
+        for k in range(len(units)):
+            add_pairs(k)
             if k == 0:
-                first(1)
-            q = k - 2
-            if 0 <= q < last:
-                quant(q)
-            if 0 <= k - 1 < last:
+                first_products(1)
+            if k >= 2:
+                quantise(k - 2)
+            if k >= 1:
                 leaky(k - 1)
-            if k == 2:
-                open_sums()
-            if k < last and k not in QV:
-                quarter(k)
+            quarter(k)
             if k < 2:
                 keep_g(k)
+            if k == 1:
+                nc.scalar.copy(out=v_cols[:], in_=columns[:, FCHUNKS : 2 * FCHUNKS])
+                for tile, factor in ((b2_relu, 0.75), (b2_quarter, 0.25), (b2_lin, 0.25 * CHUNKS[LAST][0])):
+                    nc.scalar.activation(out=tile[:], in_=columns[:, 0:FCHUNKS], func=ACT.Copy, scale=factor)
             if k == 2:
-                vt = bank("m", [P, F], BF16, "vt", 3)
-                for fc in range(4):
-                    nc.tensor.transpose(vt[:, fc * P : fc * P + P], vc[:, fc : fc + 1].to_broadcast([P, P]), ident_b[:])
-                nc.scalar.copy(out=vb[:], in_=vt[:])
-            if 0 <= q < last:
-                ci, gh = units[q]
-                if gh == 0:
-                    lin_mm(ci, 0)
-                    for fc in range(3):
-                        main_mm(ci, fc, 0)
-                elif ci < nch - 1:
-                    for fc in range(3):
-                        main_mm(ci, fc, 1)
-                        relu(ci, fc)
-                    lin_mm(ci, 1)
-                    main_mm(ci, 3, 0)
-                    main_mm(ci, 3, 1)
-                    relu(ci, 3)
-                    if ci > 0:
-                        for fc in range(4):
-                            pool(ci - 1, fc)
+                v_turned = rotating([P, F], BF16, "v_turned")
+                for fc in range(FCHUNKS):
+                    nc.tensor.transpose(
+                        v_turned[:, fc * P : fc * P + P], v_cols[:, fc : fc + 1].to_broadcast([P, P]), ident_bf[:]
+                    )
+                nc.scalar.copy(out=v_all[:], in_=v_turned[:])
+                open_sums()
+            if k >= 2:
+                second_stage(k - 2)
+        k = len(units) - 1
+        quantise(k - 1)
+        second_stage(k - 1)
+        leaky(k)
+        quantise(k)
+        second_stage(k)
+        add_up(LAST)
 
-        ci = nch - 1
-        lins = keep.tile([P, F], F32, name="lins")
-        for fc in range(4):
-            pool(ci - 1, fc)
-        for fc in range(3):
-            main_mm(ci, fc, 1)
-        relu(ci, 0, "vector")
-        relu(ci, 1)
-        relu(ci, 2, "vector")
-        lin_mm(ci, 1)
-        main_mm(ci, 3, 0)
-        main_mm(ci, 3, 1)
-        nc.scalar.activation(out=lins[:], in_=lin[0][:], func=ACT.Copy, scale=1.0 / 64.0)
-        relu(ci, 3, "vector")
-        for fc in range(4):
-            pool(ci, fc)
         pooled = keep.tile([P, F], F32, name="pooled")
-        for fc in range(4):
+        for fc in range(FCHUNKS):
+            cols = slice(fc * P, fc * P + P)
             nc.vector.scalar_tensor_tensor(
-                out=pooled[:, fc * P : fc * P + P],
-                in0=acc[fc][:],
-                scalar=3.0 / 64.0,
-                in1=lins[:, fc * P : fc * P + P],
-                op0=ALU.mult,
-                op1=ALU.add,
+                out=pooled[:, cols], in0=sums[fc][:], scalar=1.0 / N, in1=lin_mean[:, cols], op0=ALU.mult, op1=ALU.add
             )
             if fc % 2 == 1:
-                f0 = fc * P - P
+                pair = slice(fc * P - P, fc * P + P)
                 (nc.sync if fc == 1 else nc.scalar).dma_start(
-                    out=out_0.rearrange("b i f -> (b i) f")[:, f0 : f0 + 256], in_=pooled[:, f0 : f0 + 256]
+                    out=out_0.rearrange("b i f -> (b i) f")[:, pair], in_=pooled[:, pair]
                 )
-        prod = keep.tile([P, F], F32, name="prod")
+        weighted = keep.tile([P, F], F32, name="weighted")
         nc.vector.scalar_tensor_tensor(
-            out=prod[:], in0=pooled[:], scalar=1.0, in1=vb[:], op0=ALU.mult, op1=ALU.mult, accum_out=stile[:, 0:1]
+            out=weighted[:], in0=pooled[:], scalar=1.0, in1=v_all[:], op0=ALU.mult, op1=ALU.mult,
+            accum_out=score_cols[:, 0:1],
         )
-        st = bank("m", [P, P], F32, "st", 3)
-        nc.tensor.transpose(st[:], stile[:], ident[:])
-        srow = keep.tile([1, P], F32, name="srow")
-        nc.vector.tensor_copy(out=srow[:], in_=st[0:1, :])
-        nc.sync.dma_start(out=out_1.rearrange("(o b) i -> o (b i)", o=1), in_=srow[:])
+        score_turned = rotating([P, P], F32, "score_turned")
+        nc.tensor.transpose(score_turned[:], score_cols[:], ident[:])
+        score_row = keep.tile([1, P], F32, name="score_row")
+        nc.vector.tensor_copy(out=score_row[:], in_=score_turned[0:1, :])
+        nc.sync.dma_start(out=out_1.rearrange("(o b) i -> o (b i)", o=1), in_=score_row[:])

@@ -162,7 +162,7 @@ def tile_groupwisepairrankingscorer_d1p_kernel(
         nc.tensor.transpose(columns[:], rows[:], ident_bf[:])
 
         units = [(ci, half) for ci in range(len(CHUNKS)) for half in range(2)]
-        ys, quarters, zs, codes, products_of, relus = {}, {}, {}, {}, {}, {}
+        ys, quarters, zs, codes, product_banks, products_of, relus = {}, {}, {}, {}, {}, {}, {}
 
         def width(k):
             return CHUNKS[units[k][0]][1] * P * T
@@ -210,6 +210,7 @@ def tile_groupwisepairrankingscorer_d1p_kernel(
             codes[units[k]] = (words, scales)
 
         sums = []
+        pending = []
         lin = []
 
         def open_sums():
@@ -223,11 +224,11 @@ def tile_groupwisepairrankingscorer_d1p_kernel(
 
         def product(ci, fc, half):
             n = CHUNKS[ci][1] * P
-            if half == 0 and ci < LAST:
-                products_of[ci, fc] = rotating([P, PASS], F32, "product%d_%d" % (ci, fc))[:, :n]
-            elif half == 0 and fc % 2 == 0:
-                o = rotating([P, PASS], F32, "product%d_%d" % (ci, fc))
-                products_of[ci, fc], products_of[ci, fc + 1] = o[:, :n], o[:, n : 2 * n]
+            if half == 0 and (ci < LAST or fc < 3):
+                product_banks[ci, fc] = rotating([P, PASS], F32, "product%d_%d" % (ci, fc))
+                products_of[ci, fc] = product_banks[ci, fc][:, :n]
+            elif half == 0:
+                products_of[ci, fc] = product_banks[ci, fc - 1][:, n : 2 * n]
             words, scales = codes[ci, half]
             nc.tensor.matmul_mx(
                 out=products_of[ci, fc],
@@ -281,26 +282,30 @@ def tile_groupwisepairrankingscorer_d1p_kernel(
 
         def second_stage(k):
             ci, half = units[k]
-            if ci == LAST:
-                if half == 1:
-                    nc.scalar.activation(out=lin_mean[:], in_=lin[0][:], func=ACT.Copy, scale=0.25 / N)
-                    for f0 in (0, 2):
-                        for fc in (f0, f0 + 1):
-                            product(ci, fc, 0)
-                            product(ci, fc, 1)
-                        for fc in (f0, f0 + 1):
-                            activate(ci, fc)
-            elif half == 0:
-                linear(ci, 0)
+            while pending:
+                activate(*pending.pop())
+            if half == 0:
+                if ci < LAST:
+                    linear(ci, 0)
                 for fc in range(3):
                     product(ci, fc, 0)
-            else:
+            elif ci < LAST:
                 for fc in range(3):
                     product(ci, fc, 1)
                     activate(ci, fc)
                 linear(ci, 1)
                 product(ci, 3, 0)
                 product(ci, 3, 1)
+                pending.append((ci, 3))
+            else:
+                nc.scalar.activation(out=lin_mean[:], in_=lin[0][:], func=ACT.Copy, scale=0.25 / N)
+                for fc in range(2):
+                    product(ci, fc, 1)
+                    activate(ci, fc)
+                product(ci, 2, 1)
+                product(ci, 3, 0)
+                product(ci, 3, 1)
+                activate(ci, 2)
                 activate(ci, 3)
             if half == 1 and ci > 0:
                 add_up(ci - 1)

from contextlib import ExitStack

import concourse.mybir as mybir
from concourse.masks import make_identity

B, N, D, H, F = 8, 16, 1024, 1024, 512
FLOPS = 2 * (B * N) * D * H * 2 + 2 * (B * N * N) * H * F

F32 = mybir.dt.float32
BF16 = mybir.dt.bfloat16
I32 = mybir.dt.int32
U32 = mybir.dt.uint32
U8 = mybir.dt.uint8
FP8 = mybir.dt.float8_e4m3fn
FP8X4 = mybir.dt.float8_e4m3fn_x4
ALU = mybir.AluOpType
ACT = mybir.ActivationFunctionType

P = 128
T = 4
PASS = P * T
BLOCK = 128
FCHUNKS = F // P

CHUNKS = ((0, 4), (4, 4), (8, 2), (10, 2), (12, 2), (14, 2))
LAST = len(CHUNKS) - 1
UNIT = 4 * P * T


def tile_groupwisepairrankingscorer_d1p_kernel(
    tc, x_bytes, x_scale, wa_words, wa_scales, wb_words, wb_scales, c, w2_words, w2_scales, b2, v, out_0, out_1
):
    nc = tc.nc
    with ExitStack() as ctx:
        keep = ctx.enter_context(tc.tile_pool(name="keep", bufs=1))
        work = ctx.enter_context(tc.tile_pool(name="work", bufs=3))
        psum = ctx.enter_context(tc.psum_pool(name="psum", bufs=1))
        ctx.enter_context(tc.manual_schedule())

        def rotating(shape, dtype, name):
            return psum.tile(shape, dtype, tag="m", name=name, bufs=3)

        def fixed(tag, shape, dtype, name):
            return psum.tile(shape, dtype, tag=tag, name=name, bufs=1)

        x_codes8 = keep.tile([P, D], U8, name="x_codes8", align_bytes=64)
        x_scales = keep.tile([P, D // BLOCK], F32, name="x_scales")
        nc.sync.dma_start(out=x_scales[:], in_=x_scale.rearrange("b n q -> (b n) q"))
        nc.sync.dma_start(out=x_codes8[:], in_=x_bytes.rearrange("b n k -> (b n) k"))

        rows = keep.tile([P, P], BF16, name="rows")
        nc.vector.memset(rows[:], 0.0)
        score_cols = keep.tile([P, P], F32, name="score_cols")
        nc.scalar.activation(out=score_cols[:], in_=rows[:], func=ACT.Relu)
        w1_scales = [keep.tile([P, 2, H], U8, name="w1_scales%d" % w, align_bytes=64) for w in range(2)]
        for w in range(2):
            nc.vector.memset(w1_scales[w][:].bitcast(I32), 0)
        w2_scale = keep.tile([P, 2, F], U8, name="w2_scale", align_bytes=64)
        nc.vector.memset(w2_scale[:].bitcast(I32), 0)

        ident = keep.tile([P, P], F32, name="ident")
        make_identity(nc, ident[:])

        w1_codes = [
            [keep.tile([P, 2, PASS], U32, name="w1_codes%d_%d" % (w, half), align_bytes=64) for half in range(2)]
            for w in range(2)
        ]

        def load_w1(words, w, half):
            nc.sync.dma_start(
                out=w1_codes[w][half][:].bitcast(I32),
                in_=words.bitcast(I32).rearrange("g p n o -> p g (n o)")[:, :, half * PASS : half * PASS + PASS],
            )

        def load_scales(queue, dst, src):
            for r in range(4):
                queue.dma_start(
                    out=dst[r:P:32, :, :].bitcast(I32),
                    in_=src.bitcast(I32)[:, r:16:4, :].rearrange("g q n -> q g n"),
                )

        load_scales(nc.sync, w1_scales[0], wa_scales)
        load_w1(wa_words, 0, 0)
        load_w1(wb_words, 1, 0)
        load_scales(nc.sync, w1_scales[1], wb_scales)
        load_w1(wa_words, 0, 1)
        load_w1(wb_words, 1, 1)
        w2_codes = keep.tile([P, 2, F], U32, name="w2_codes", align_bytes=64)
        nc.sync.dma_start(out=w2_codes[:].bitcast(I32), in_=w2_words.bitcast(I32).rearrange("g p n o -> p g (n o)"))
        c_cols = keep.tile([P, 2, T], BF16, name="c_cols")
        nc.gpsimd.dma_start(out=c_cols[:], in_=c.rearrange("(g p t) -> p g t", g=2, t=T))
        nc.gpsimd.dma_start(out=rows[0:FCHUNKS, :], in_=b2.rearrange("(c p) -> c p", p=P))
        nc.gpsimd.dma_start(out=rows[FCHUNKS : 2 * FCHUNKS, :], in_=v.rearrange("(c p) -> c p", p=P))
        load_scales(nc.gpsimd, w2_scale, w2_scales)

        x_wide = keep.tile([P, D], BF16, name="x_wide", align_bytes=64)
        for q in range(D // BLOCK):
            cols = slice(q * BLOCK, q * BLOCK + BLOCK)
            src = x_codes8[:, cols].bitcast(FP8)
            scale = x_scales[:, q : q + 1]
            if q % 2 == 0:
                nc.vector.tensor_scalar(out=x_wide[:, cols], in0=src, scalar1=scale, scalar2=None, op0=ALU.mult)
            else:
                nc.scalar.activation(out=x_wide[:, cols], in_=src, func=ACT.Copy, scale=scale)

        x_words = x_wide[:].bitcast(F32)
        x_turned = [rotating([P, 2, P], F32, "x_turned%d" % g) for g in range(2)]
        for g in range(2):
            for u in range(2):
                nc.tensor.transpose(x_turned[g][:, u, :], x_words[:, 256 * g + u : 256 * g + 256 : 2], ident[:])
        x_grouped = keep.tile([P, 2, P, T], BF16, name="x_grouped", align_bytes=64)
        nc.vector.tensor_copy(out=x_grouped[:, 0].bitcast(F32), in_=x_turned[0][:].rearrange("p u d -> p d u"))
        nc.scalar.copy(out=x_grouped[:, 1].bitcast(F32), in_=x_turned[1][:].rearrange("p u d -> p d u"))
        ident_bf = keep.tile([P, P], BF16, name="ident_bf")
        nc.vector.tensor_copy(out=ident_bf[:], in_=ident[:])
        x_codes = keep.tile([P, 2, P], U32, name="x_codes", align_bytes=64)
        x_mx_scales = keep.tile([P, 2, P], U8, name="x_mx_scales", align_bytes=64)
        for g in range(2):
            nc.vector.quantize_mx(
                out=x_codes[:, g, :].bitcast(FP8X4),
                scales=x_mx_scales[:, g, :],
                in_=x_grouped[:, g].rearrange("p d t -> p (d t)"),
            )

        by_doc = [[keep.tile([P, T, P], F32, name="by_doc%d_%d" % (w, half)) for half in range(2)] for w in range(2)]
        a_c = [keep.tile([P, P, T], F32, name="a_c%d" % half) for half in range(2)]
        g_kept = [keep.tile([P, P, T], F32, name="g_kept%d" % half) for half in range(2)]
        g_psum = {}
        ident_jb = ident[:].rearrange("p (b j) -> p j b", b=B)

        def first_products(half):
            banks = []
            for w in range(2):
                o = rotating([P, PASS], F32, "first%d_%d" % (w, half))
                for g in range(2):
                    nc.tensor.matmul_mx(
                        out=o[:],
                        lhsT=x_codes[:, g, :].bitcast(FP8X4),
                        lhsT_scale=x_mx_scales[:, g, :],
                        rhs=w1_codes[w][half][:, g, :].bitcast(FP8X4),
                        rhs_scale=w1_scales[w][:, g, half * PASS : half * PASS + PASS],
                        start=g == 0,
                        stop=g == 1,
                    )
                banks.append(o)
            for w in range(2):
                nc.scalar.copy(out=by_doc[w][half][:], in_=banks[w][:].rearrange("p (m t) -> p t m", t=T))
            turned = []
            for w in range(2):
                o = fixed("acc%d" % (2 * half + w), [P, T, P], F32, "turned%d_%d" % (w, half))
                for t in range(T):
                    nc.tensor.transpose(o[:, t, :], by_doc[w][half][:, t, :], ident_jb if w == 1 else ident[:])
                turned.append(o[:].rearrange("p t d -> p d t"))
            nc.vector.tensor_tensor(
                out=a_c[half][:], in0=turned[0], in1=c_cols[:, half, :].unsqueeze(1).to_broadcast([P, P, T]), op=ALU.add
            )
            g_psum[half] = turned[1]

        first_products(0)

        columns = fixed("lin", [P, P], BF16, "columns")
        nc.tensor.transpose(columns[:], rows[:], ident_bf[:])

        units = [(ci, half) for ci in range(len(CHUNKS)) for half in range(2)]
        ys, quarters, zs, codes, product_banks, products_of, relus = {}, {}, {}, {}, {}, {}, {}

        def width(k):
            return CHUNKS[units[k][0]][1] * P * T

        def add_pairs(k):
            ci, half = units[k]
            j0, jn = CHUNKS[ci]
            ys[k] = work.tile([P, UNIT], BF16, tag="y", name="y%d" % k, bufs=4, align_bytes=64)
            g = g_psum.get(half, g_kept[half][:])
            nc.vector.tensor_tensor(
                out=ys[k][:, : width(k)].rearrange("p (j b i t) -> p j b i t", j=jn, b=B, t=T),
                in0=a_c[half][:]
                .rearrange("p (b i) t -> p b i t", b=B)
                .unsqueeze(1)
                .to_broadcast([P, jn, B, N, T]),
                in1=g.rearrange("p (j b) t -> p j b t", b=B)[:, j0 : j0 + jn]
                .unsqueeze(3)
                .to_broadcast([P, jn, B, N, T]),
                op=ALU.add,
            )

        def keep_g(half):
            nc.scalar.copy(out=g_kept[half][:], in_=g_psum.pop(half))

        def quarter(k):
            quarters[k] = work.tile([P, UNIT], BF16, tag="quarter", name="quarter%d" % k, bufs=3, align_bytes=64)
            out, src = quarters[k][:, : width(k)], ys[k][:, : width(k)]
            if k == len(units) - 1:
                nc.vector.tensor_scalar(out=out, in0=src, scalar1=0.25, scalar2=None, op0=ALU.mult)
            else:
                nc.scalar.activation(out=out, in_=src, func=ACT.Copy, scale=0.25)

        def leaky(k):
            w = width(k)
            zs[k] = work.tile([P, UNIT], BF16, tag="z", name="z%d" % k, bufs=3, align_bytes=64)
            nc.vector.tensor_tensor(out=zs[k][:, :w], in0=ys[k][:, :w], in1=quarters[k][:, :w], op=ALU.max)

        def quantise(k):
            n = width(k) // T
            words = work.tile([P, UNIT // T], U32, tag="z_words", name="z_words%d" % k, bufs=5, align_bytes=64)
            scales = work.tile([P, UNIT // T], U8, tag="z_scales", name="z_scales%d" % k, bufs=5, align_bytes=64)
            nc.vector.quantize_mx(
                out=words[:, :n].bitcast(FP8X4), scales=scales[:, :n], in_=zs[k][:, : width(k)]
            )
            codes[units[k]] = (words, scales)

        sums = []
        pending = []
        lin = []

        def open_sums():
            for fc in range(FCHUNKS):
                sums.append(fixed("acc%d" % fc, [P, P], F32, "sum%d" % fc))
                nc.tensor.matmul(
                    sums[fc][:], b2_lin[:, fc : fc + 1].to_broadcast([P, P]), ident[:],
                    is_transpose=True, start=True, stop=False,
                )
            lin.append(fixed("lin", [P, F], F32, "lin"))

        def product(ci, fc, half):
            n = CHUNKS[ci][1] * P
            if half == 0 and (ci < LAST or fc < 3):
                product_banks[ci, fc] = rotating([P, PASS], F32, "product%d_%d" % (ci, fc))
                products_of[ci, fc] = product_banks[ci, fc][:, :n]
            elif half == 0:
                products_of[ci, fc] = product_banks[ci, fc - 1][:, n : 2 * n]
            words, scales = codes[ci, half]
            nc.tensor.matmul_mx(
                out=products_of[ci, fc],
                lhsT=w2_codes[:, half, fc * P : fc * P + P].bitcast(FP8X4),
                lhsT_scale=w2_scale[:, half, fc * P : fc * P + P],
                rhs=words[:, :n].bitcast(FP8X4),
                rhs_scale=scales[:, :n],
                start=half == 0,
                stop=half == 1,
            )

        def linear(ci, half):
            words, scales = codes[ci, half]
            for j in range(CHUNKS[ci][1]):
                cols = slice(j * P, j * P + P)
                nc.tensor.matmul_mx(
                    out=lin[0][:],
                    lhsT=words[:, cols].bitcast(FP8X4),
                    lhsT_scale=scales[:, cols],
                    rhs=w2_codes[:, half, :].bitcast(FP8X4),
                    rhs_scale=w2_scale[:, half, :],
                    start=ci == 0 and j == 0 and half == 0,
                    stop=ci == LAST - 1 and j == CHUNKS[ci][1] - 1 and half == 1,
                )

        def activate(ci, fc):
            n = CHUNKS[ci][1] * P
            r = work.tile([P, PASS], F32, tag="relu", name="relu%d_%d" % (ci, fc), bufs=16)
            relus[ci, fc] = r
            if ci < LAST:
                nc.scalar.activation(
                    out=r[:, :n], in_=products_of[ci, fc], func=ACT.Relu, scale=0.75, bias=b2_relu[:, fc : fc + 1]
                )
            else:
                u = work.tile([P, PASS], F32, tag="u", name="u%d" % fc, bufs=4)
                nc.scalar.activation(
                    out=u[:, :n], in_=products_of[ci, fc], func=ACT.Identity, scale=0.25, bias=b2_quarter[:, fc : fc + 1]
                )
                nc.vector.scalar_tensor_tensor(
                    out=r[:, :n], in0=u[:, :n], scalar=4.0, in1=u[:, :n], op0=ALU.mult, op1=ALU.max
                )

        def add_up(ci):
            jn = CHUNKS[ci][1]
            for fc in range(FCHUNKS):
                for j in range(jn):
                    nc.tensor.matmul(
                        sums[fc][:], relus[ci, fc][:, j * P : j * P + P], ident[:],
                        is_transpose=True, start=False, stop=ci == LAST and j == jn - 1,
                    )

        def second_stage(k):
            ci, half = units[k]
            while pending:
                activate(*pending.pop())
            if half == 0:
                if ci < LAST:
                    linear(ci, 0)
                for fc in range(3):
                    product(ci, fc, 0)
            elif ci < LAST:
                for fc in range(3):
                    product(ci, fc, 1)
                    activate(ci, fc)
                linear(ci, 1)
                product(ci, 3, 0)
                product(ci, 3, 1)
                pending.append((ci, 3))
            else:
                nc.scalar.activation(out=lin_mean[:], in_=lin[0][:], func=ACT.Copy, scale=0.25 / N)
                for fc in range(2):
                    product(ci, fc, 1)
                    activate(ci, fc)
                product(ci, 2, 1)
                product(ci, 3, 0)
                product(ci, 3, 1)
                activate(ci, 2)
                activate(ci, 3)
            if half == 1 and ci > 0:
                add_up(ci - 1)

        b2_relu = keep.tile([P, FCHUNKS], F32, name="b2_relu")
        b2_quarter = keep.tile([P, FCHUNKS], F32, name="b2_quarter")
        b2_lin = keep.tile([P, FCHUNKS], F32, name="b2_lin")
        v_cols = keep.tile([P, FCHUNKS], BF16, name="v_cols")
        v_all = keep.tile([P, F], BF16, name="v_all")
        lin_mean = keep.tile([P, F], F32, name="lin_mean")

        for k in range(len(units)):
            add_pairs(k)
            if k == 0:
                first_products(1)
            if k >= 2:
                quantise(k - 2)
            if k >= 1:
                leaky(k - 1)
            quarter(k)
            if k < 2:
                keep_g(k)
            if k == 1:
                nc.scalar.copy(out=v_cols[:], in_=columns[:, FCHUNKS : 2 * FCHUNKS])
                for tile, factor in ((b2_relu, 0.75), (b2_quarter, 0.25), (b2_lin, 0.25 * CHUNKS[LAST][0])):
                    nc.scalar.activation(out=tile[:], in_=columns[:, 0:FCHUNKS], func=ACT.Copy, scale=factor)
            if k == 2:
                v_turned = rotating([P, F], BF16, "v_turned")
                for fc in range(FCHUNKS):
                    nc.tensor.transpose(
                        v_turned[:, fc * P : fc * P + P], v_cols[:, fc : fc + 1].to_broadcast([P, P]), ident_bf[:]
                    )
                nc.scalar.copy(out=v_all[:], in_=v_turned[:])
                open_sums()
            if k >= 2:
                second_stage(k - 2)
        k = len(units) - 1
        quantise(k - 1)
        second_stage(k - 1)
        leaky(k)
        quantise(k)
        second_stage(k)
        add_up(LAST)

        pooled = keep.tile([P, F], F32, name="pooled")
        for fc in range(FCHUNKS):
            cols = slice(fc * P, fc * P + P)
            nc.vector.scalar_tensor_tensor(
                out=pooled[:, cols], in0=sums[fc][:], scalar=1.0 / N, in1=lin_mean[:, cols], op0=ALU.mult, op1=ALU.add
            )
            if fc % 2 == 1:
                pair = slice(fc * P - P, fc * P + P)
                (nc.sync if fc == 1 else nc.scalar).dma_start(
                    out=out_0.rearrange("b i f -> (b i) f")[:, pair], in_=pooled[:, pair]
                )
        weighted = keep.tile([P, F], F32, name="weighted")
        nc.vector.scalar_tensor_tensor(
            out=weighted[:], in0=pooled[:], scalar=1.0, in1=v_all[:], op0=ALU.mult, op1=ALU.mult,
            accum_out=score_cols[:, 0:1],
        )
        score_turned = rotating([P, P], F32, "score_turned")
        nc.tensor.transpose(score_turned[:], score_cols[:], ident[:])
        score_row = keep.tile([1, P], F32, name="score_row")
        nc.vector.tensor_copy(out=score_row[:], in_=score_turned[0:1, :])
        nc.sync.dma_start(out=out_1.rearrange("(o b) i -> o (b i)", o=1), in_=score_row[:])
